import numpy as np
import ml_dtypes


def mxq(x, axis, fmt="e4m3"):
    dtype, down = {"e4m3": (ml_dtypes.float8_e4m3fn, 7), "e5m2": (ml_dtypes.float8_e5m2, 14)}[fmt]
    v = np.moveaxis(np.asarray(x, np.float32).astype(ml_dtypes.bfloat16).astype(np.float64), axis, -1)
    blocks = v.reshape(v.shape[:-1] + (-1, 32))
    amax = np.abs(blocks).max(-1, keepdims=True)
    byte = np.maximum(np.where(amax > 0, np.frexp(amax)[1] - 1 + 127, 0) - down, 1)
    scale = np.exp2(byte - 127.0)
    codes = (blocks / scale).astype(np.float32).astype(dtype).astype(np.float64)
    return np.moveaxis((codes * scale).reshape(v.shape), -1, axis)


WIDE = False


def mx_kscale(k):
    if not WIDE:
        return np.ones(k)
    levels = np.array([10, -10, 5, -5, 0])
    if k % 512:
        return np.exp2(np.random.permutation(np.resize(levels, k // 32))).repeat(32)
    a = np.empty((k // 512, 16))
    for p in range(k // 512):
        a[p, :8] = np.random.permutation(np.resize(levels, 8))
        for g in range(8):
            far = levels[np.abs(levels - a[p, g]) >= 10]
            a[p, g + 8] = far[np.random.randint(len(far))]
    return np.exp2(a.ravel()).repeat(32)


def f64(x):
    return np.asarray(x).astype(np.float64)


E2M1 = np.array([0.0, 0.5, 1.0, 1.5, 2.0, 3.0, 4.0, 6.0, -0.0, -0.5, -1.0, -1.5, -2.0, -3.0, -4.0, -6.0])


def pack_weight(w, fmt):
    k, n = w.shape
    w = f64(np.asarray(w, np.float32).astype(ml_dtypes.bfloat16)).reshape(k // 32, 32, n)
    amax = np.abs(w).max(1)
    if fmt == "e4m3":
        byte = np.frexp(amax)[1] - 1 + 127 - 7
    else:
        mant, ex = np.frexp(amax / 6.0)
        byte = np.where(mant > 0.5, ex, ex - 1) + 127
    byte = np.clip(np.where(amax > 0, byte, 1), 1, 254)
    scaled = (w * np.exp2(127.0 - byte)[:, None, :]).reshape(k, n).astype(np.float32)
    by_word = np.ascontiguousarray(scaled.reshape(k // 512, 128, 4, n).transpose(0, 1, 3, 2))
    if fmt == "e4m3":
        words = by_word.astype(ml_dtypes.float8_e4m3fn).view(np.uint8)
    else:
        c = by_word.astype(ml_dtypes.float4_e2m1fn).view(np.uint8) & 0xF
        words = (c[..., 0::2] | (c[..., 1::2] << 4)).reshape(k // 512, 128, 2 * n)
    return np.ascontiguousarray(words), np.ascontiguousarray(byte.astype(np.uint8).reshape(k // 512, 16, n))


def unpack_weight(words, scales, fmt):
    g, _, n = scales.shape
    words = np.ascontiguousarray(words).reshape(g, 128, n, -1)
    if fmt == "e4m3":
        vals = words.view(ml_dtypes.float8_e4m3fn).astype(np.float64)
    else:
        nib = np.empty((g, 128, n, 4), np.uint8)
        nib[..., 0::2] = words & 0xF
        nib[..., 1::2] = words >> 4
        vals = E2M1[nib]
    vals = vals * np.repeat(np.exp2(scales.astype(np.float64) - 127.0), 8, axis=1)[..., None]
    return vals.transpose(0, 1, 3, 2).reshape(g * 512, n)


O, T, D, Q = 512, 1024, 1024, 512


def setup_inputs():
    n = np.random.standard_normal
    s = mx_kscale(T)[:, None]
    v = n((T, D)) / s
    l = 1.5 * n((T, Q))
    p_v4 = pack_weight(v[:O], "e2m1")
    p_v8 = pack_weight(v[O:], "e4m3")
    return {
        "lg": (l - l.max(0)).astype(np.float32),
        "vs": (np.random.uniform(0.5, 2.0, T) * s[:, 0]).astype(np.float32),
        "v4_words": p_v4[0],
        "v4_scales": p_v4[1],
        "v8_words": p_v8[0],
        "v8_scales": p_v8[1],
    }


def reference(lg, vs, v4_words, v4_scales, v8_words, v8_scales):
    e_ = mxq(np.exp(f64(lg)) * f64(vs)[:, None], 0, "e4m3")
    v4_ = unpack_weight(v4_words, v4_scales, "e2m1")
    v8_ = unpack_weight(v8_words, v8_scales, "e4m3")
    y = e_[:O].T @ v4_ + e_[O:].T @ v8_
    return y

@@ -1,0 +1,136 @@
+from contextlib import ExitStack
+
+import concourse.mybir as mybir
+
+T, J, D = 1024, 512, 1024
+P = 128
+PACK = 4
+HALF = P * PACK
+J_TILE = 128
+N_TILE = 512
+
+FLOPS = 2 * T * J * D
+
+F32 = mybir.dt.float32
+BF16 = mybir.dt.bfloat16
+I32 = mybir.dt.int32
+U32 = mybir.dt.uint32
+U8 = mybir.dt.uint8
+FP8X4 = mybir.dt.float8_e4m3fn_x4
+FP4X4 = mybir.dt.float4_e2m1fn_x4
+EXP = mybir.ActivationFunctionType.Exp
+MULT = mybir.AluOpType.mult
+
+
+def tile_mix_kvmix_tm_none_kernel(tc, lg, vs, v4_words, v4_scales, v8_words, v8_scales, out):
+    nc = tc.nc
+    j_tiles = J // J_TILE
+    n_tiles = D // N_TILE
+
+    with ExitStack() as ctx:
+        keep = ctx.enter_context(tc.tile_pool(name="keep", bufs=1))
+        psum = ctx.enter_context(tc.psum_pool(name="psum", bufs=1))
+        ctx.enter_context(tc.manual_schedule())
+
+        warm = keep.tile([P, 1], F32, name="warm")
+        warmed = keep.tile([P, 1], F32, name="warmed")
+        vs_sb = keep.tile([P, 2, PACK], F32, name="vs_sb")
+        logits = [keep.tile([P, PACK, J], F32, name="logits%d" % h) for h in range(2)]
+        exps = [keep.tile([P, PACK, J], F32, name="exps%d" % h) for h in range(2)]
+        grouped = [keep.tile([P, J * PACK], BF16, name="grouped%d" % h, align_bytes=64) for h in range(2)]
+        e_codes = [keep.tile([P, J], U32, name="e_codes%d" % h, align_bytes=64) for h in range(2)]
+        e_scales = [keep.tile([P, J], U8, name="e_scales%d" % h, align_bytes=64) for h in range(2)]
+        v4_sb = keep.tile([P, 2 * D], U8, name="v4_sb", align_bytes=64)
+        v8_sb = keep.tile([P, D], U32, name="v8_sb", align_bytes=64)
+        v_scales = [keep.tile([P, D], U8, name="v_scales%d" % h, align_bytes=64) for h in range(2)]
+        results = [keep.tile([P, D], F32, name="results%d" % j) for j in range(j_tiles)]
+        accs = [
+            [psum.tile([P, N_TILE], F32, name="acc%d_%d" % (j, n)) for n in range(n_tiles)] for j in range(j_tiles)
+        ]
+
+        def load_logits(h, j0, j1):
+            rows = lg[h * HALF : (h + 1) * HALF, j0:j1].rearrange("(p i) j -> p i j", i=PACK)
+            nc.sync.dma_start(out=logits[h][:, :, j0:j1], in_=rows)
+
+        def load_scales(engine, h, scales):
+            for q in range(4):
+                engine.dma_start(
+                    out=v_scales[h][32 * q : 32 * q + 4, :].bitcast(I32),
+                    in_=scales[0, 4 * q : 4 * q + 4, :].bitcast(I32),
+                )
+
+        nc.vector.memset(warm[:], 0.0)
+        nc.vector.memset(v_scales[0][:].bitcast(I32), 0)
+        nc.vector.memset(v_scales[1][:].bitcast(I32), 0)
+        nc.scalar.dma_start(out=vs_sb[:], in_=vs.rearrange("(h p i) -> p h i", h=2, i=PACK))
+        load_logits(0, 0, 384)
+        load_logits(1, 0, 384)
+        load_scales(nc.gpsimd, 0, v4_scales)
+        load_scales(nc.scalar, 1, v8_scales)
+        nc.scalar.activation(out=warmed[:], in_=warm[:], func=EXP)
+        nc.sync.dma_start(out=v4_sb[:].bitcast(I32), in_=v4_words[0].bitcast(I32))
+        nc.sync.dma_start(out=v8_sb[:].bitcast(I32), in_=v8_words[0].rearrange("p n t -> p (n t)").bitcast(I32))
+        load_logits(0, 384, 512)
+        load_logits(1, 384, 512)
+
+        def exponentiate(h, j):
+            cols = slice(j * J_TILE, (j + 1) * J_TILE)
+            nc.scalar.activation(out=exps[h][:, :, cols], in_=logits[h][:, :, cols], func=EXP)
+
+        def scale(h, j):
+            cols = slice(j * J_TILE, (j + 1) * J_TILE)
+            words = slice(PACK * j * J_TILE, PACK * (j + 1) * J_TILE)
+            factor = vs_sb[:, h, :].unsqueeze(1).unsqueeze(3).to_broadcast([P, J_TILE // 2, PACK, 2])
+            nc.vector.tensor_tensor(
+                out=grouped[h][:, words].rearrange("p (c u i) -> p c i u", u=2, i=PACK),
+                in0=exps[h][:, :, cols].rearrange("p i (c u) -> p c i u", u=2),
+                in1=factor,
+                op=MULT,
+            )
+
+        def quantize(h, j):
+            cols = slice(j * J_TILE, (j + 1) * J_TILE)
+            words = slice(PACK * j * J_TILE, PACK * (j + 1) * J_TILE)
+            nc.vector.quantize_mx(
+                out=e_codes[h][:, cols].bitcast(FP8X4), scales=e_scales[h][:, cols], in_=grouped[h][:, words]
+            )
+
+        def multiply(h, j):
+            cols = slice(j * J_TILE, (j + 1) * J_TILE)
+            for n in range(n_tiles):
+                if h == 0:
+                    moving = v4_sb[:, 2 * n * N_TILE : 2 * (n + 1) * N_TILE].bitcast(FP4X4)
+                else:
+                    moving = v8_sb[:, n * N_TILE : (n + 1) * N_TILE].bitcast(FP8X4)
+                nc.tensor.matmul_mx(
+                    out=accs[j][n][:],
+                    lhsT=e_codes[h][:, cols].bitcast(FP8X4),
+                    lhsT_scale=e_scales[h][:, cols],
+                    rhs=moving,
+                    rhs_scale=v_scales[h][:, n * N_TILE : (n + 1) * N_TILE],
+                    start=(h == 0),
+                    stop=(h == 1),
+                )
+
+        def drain(j):
+            for n in range(n_tiles):
+                cols = slice(n * N_TILE, (n + 1) * N_TILE)
+                if n == 0 or j == 0:
+                    nc.scalar.copy(out=results[j][:, cols], in_=accs[j][n][:])
+                else:
+                    nc.vector.tensor_copy(out=results[j][:, cols], in_=accs[j][n][:])
+                nc.sync.dma_start(out=out[j * J_TILE : (j + 1) * J_TILE, cols], in_=results[j][:, cols])
+
+        units = [(0, 0), (0, 1), (0, 2), (1, 0), (1, 1), (1, 2), (0, 3), (1, 3)]
+        for s in range(len(units) + 3):
+            if s < len(units):
+                exponentiate(*units[s])
+            if 1 <= s <= len(units):
+                scale(*units[s - 1])
+            if 2 <= s <= len(units) + 1:
+                quantize(*units[s - 2])
+                multiply(*units[s - 2])
+            if s >= 3:
+                h, j = units[s - 3]
+                if h == 1:
+                    drain(j)

@@ -62,75 +62,110 @@ def tile_mix_kvmix_tm_none_kernel(tc, lg, vs, v4_words, v4_scales, v8_words, v8_
         nc.vector.memset(warm[:], 0.0)
         nc.vector.memset(v_scales[0][:].bitcast(I32), 0)
         nc.vector.memset(v_scales[1][:].bitcast(I32), 0)
+        def load_v8(n):
+            cols = slice(n * N_TILE, (n + 1) * N_TILE)
+            nc.sync.dma_start(
+                out=v8_sb[:, cols].bitcast(I32),
+                in_=v8_words[0].rearrange("p n t -> p (n t)")[:, 4 * n * N_TILE : 4 * (n + 1) * N_TILE].bitcast(I32),
+            )
+
         nc.scalar.dma_start(out=vs_sb[:], in_=vs.rearrange("(h p i) -> p h i", h=2, i=PACK))
         load_logits(0, 0, 384)
-        load_logits(1, 0, 384)
-        load_scales(nc.gpsimd, 0, v4_scales)
-        load_scales(nc.scalar, 1, v8_scales)
+        load_scales(nc.scalar, 0, v4_scales)
+        load_scales(nc.gpsimd, 1, v8_scales)
         nc.scalar.activation(out=warmed[:], in_=warm[:], func=EXP)
+        load_logits(1, 0, 384)
         nc.sync.dma_start(out=v4_sb[:].bitcast(I32), in_=v4_words[0].bitcast(I32))
-        nc.sync.dma_start(out=v8_sb[:].bitcast(I32), in_=v8_words[0].rearrange("p n t -> p (n t)").bitcast(I32))
         load_logits(0, 384, 512)
+        load_v8(0)
+        load_v8(1)
         load_logits(1, 384, 512)
 
-        def exponentiate(h, j):
-            cols = slice(j * J_TILE, (j + 1) * J_TILE)
-            nc.scalar.activation(out=exps[h][:, :, cols], in_=logits[h][:, :, cols], func=EXP)
+        def cols(j0, j1, per=1):
+            return slice(per * j0 * J_TILE, per * j1 * J_TILE)
 
-        def scale(h, j):
-            cols = slice(j * J_TILE, (j + 1) * J_TILE)
-            words = slice(PACK * j * J_TILE, PACK * (j + 1) * J_TILE)
-            factor = vs_sb[:, h, :].unsqueeze(1).unsqueeze(3).to_broadcast([P, J_TILE // 2, PACK, 2])
+        def exponentiate(h, j0, j1):
+            nc.scalar.activation(out=exps[h][:, :, cols(j0, j1)], in_=logits[h][:, :, cols(j0, j1)], func=EXP)
+
+        def scale(h, j0, j1):
+            pairs = (j1 - j0) * J_TILE // 2
+            factor = vs_sb[:, h, :].unsqueeze(1).unsqueeze(3).to_broadcast([P, pairs, PACK, 2])
             nc.vector.tensor_tensor(
-                out=grouped[h][:, words].rearrange("p (c u i) -> p c i u", u=2, i=PACK),
-                in0=exps[h][:, :, cols].rearrange("p i (c u) -> p c i u", u=2),
+                out=grouped[h][:, cols(j0, j1, PACK)].rearrange("p (c u i) -> p c i u", u=2, i=PACK),
+                in0=exps[h][:, :, cols(j0, j1)].rearrange("p i (c u) -> p c i u", u=2),
                 in1=factor,
                 op=MULT,
             )
 
-        def quantize(h, j):
-            cols = slice(j * J_TILE, (j + 1) * J_TILE)
-            words = slice(PACK * j * J_TILE, PACK * (j + 1) * J_TILE)
+        def quantize(h, j0, j1):
             nc.vector.quantize_mx(
-                out=e_codes[h][:, cols].bitcast(FP8X4), scales=e_scales[h][:, cols], in_=grouped[h][:, words]
+                out=e_codes[h][:, cols(j0, j1)].bitcast(FP8X4),
+                scales=e_scales[h][:, cols(j0, j1)],
+                in_=grouped[h][:, cols(j0, j1, PACK)],
             )
 
-        def multiply(h, j):
-            cols = slice(j * J_TILE, (j + 1) * J_TILE)
-            for n in range(n_tiles):
-                if h == 0:
-                    moving = v4_sb[:, 2 * n * N_TILE : 2 * (n + 1) * N_TILE].bitcast(FP4X4)
-                else:
-                    moving = v8_sb[:, n * N_TILE : (n + 1) * N_TILE].bitcast(FP8X4)
-                nc.tensor.matmul_mx(
-                    out=accs[j][n][:],
-                    lhsT=e_codes[h][:, cols].bitcast(FP8X4),
-                    lhsT_scale=e_scales[h][:, cols],
-                    rhs=moving,
-                    rhs_scale=v_scales[h][:, n * N_TILE : (n + 1) * N_TILE],
-                    start=(h == 0),
-                    stop=(h == 1),
-                )
+        def multiply(h, j0, j1):
+            for j in range(j0, j1):
+                for n in range(n_tiles):
+                    if h == 0:
+                        moving = v4_sb[:, 2 * n * N_TILE : 2 * (n + 1) * N_TILE].bitcast(FP4X4)
+                    else:
+                        moving = v8_sb[:, n * N_TILE : (n + 1) * N_TILE].bitcast(FP8X4)
+                    nc.tensor.matmul_mx(
+                        out=accs[j][n][:],
+                        lhsT=e_codes[h][:, cols(j, j + 1)].bitcast(FP8X4),
+                        lhsT_scale=e_scales[h][:, cols(j, j + 1)],
+                        rhs=moving,
+                        rhs_scale=v_scales[h][:, n * N_TILE : (n + 1) * N_TILE],
+                        start=(h == 0),
+                        stop=(h == 1),
+                    )
 
-        def drain(j):
-            for n in range(n_tiles):
-                cols = slice(n * N_TILE, (n + 1) * N_TILE)
-                if n == 0 or j == 0:
-                    nc.scalar.copy(out=results[j][:, cols], in_=accs[j][n][:])
-                else:
-                    nc.vector.tensor_copy(out=results[j][:, cols], in_=accs[j][n][:])
-                nc.sync.dma_start(out=out[j * J_TILE : (j + 1) * J_TILE, cols], in_=results[j][:, cols])
+        def drain(j, n, engine):
+            d_cols = slice(n * N_TILE, (n + 1) * N_TILE)
+            if engine == "scalar":
+                nc.scalar.copy(out=results[j][:, d_cols], in_=accs[j][n][:])
+            else:
+                nc.vector.tensor_copy(out=results[j][:, d_cols], in_=accs[j][n][:])
+            nc.sync.dma_start(out=out[j * J_TILE : (j + 1) * J_TILE, d_cols], in_=results[j][:, d_cols])
 
-        units = [(0, 0), (0, 1), (0, 2), (1, 0), (1, 1), (1, 2), (0, 3), (1, 3)]
-        for s in range(len(units) + 3):
-            if s < len(units):
-                exponentiate(*units[s])
-            if 1 <= s <= len(units):
-                scale(*units[s - 1])
-            if 2 <= s <= len(units) + 1:
-                quantize(*units[s - 2])
-                multiply(*units[s - 2])
-            if s >= 3:
-                h, j = units[s - 3]
-                if h == 1:
-                    drain(j)
+        exponentiate(0, 0, 1)
+        exponentiate(0, 1, 2)
+        scale(0, 0, 1)
+        exponentiate(0, 2, 3)
+        scale(0, 1, 2)
+        quantize(0, 0, 1)
+        multiply(0, 0, 1)
+        exponentiate(1, 0, 1)
+        scale(0, 2, 3)
+        quantize(0, 1, 2)
+        multiply(0, 1, 2)
+        exponentiate(1, 1, 2)
+        quantize(0, 2, 3)
+        multiply(0, 2, 3)
+        scale(1, 0, 1)
+        exponentiate(1, 2, 3)
+        scale(1, 1, 2)
+        quantize(1, 0, 1)
+        multiply(1, 0, 1)
+        exponentiate(0, 3, 4)
+        scale(1, 2, 3)
+        quantize(1, 1, 2)
+        multiply(1, 1, 2)
+        drain(0, 0, "scalar")
+        scale(0, 3, 4)
+        quantize(1, 2, 3)
+        multiply(1, 2, 3)
+        drain(0, 1, "scalar")
+        exponentiate(1, 3, 4)
+        quantize(0, 3, 4)
+        multiply(0, 3, 4)
+        drain(1, 0, "vector")
+        scale(1, 3, 4)
+        drain(1, 1, "scalar")
+        drain(2, 0, "vector")
+        quantize(1, 3, 4)
+        multiply(1, 3, 4)
+        drain(2, 1, "scalar")
+        drain(3, 0, "vector")
+        drain(3, 1, "scalar")

@@ -72,10 +72,10 @@ def tile_mix_kvmix_tm_none_kernel(tc, lg, vs, v4_words, v4_scales, v8_words, v8_
         nc.scalar.dma_start(out=vs_sb[:], in_=vs.rearrange("(h p i) -> p h i", h=2, i=PACK))
         load_logits(0, 0, 384)
         load_scales(nc.scalar, 0, v4_scales)
-        load_scales(nc.gpsimd, 1, v8_scales)
         nc.scalar.activation(out=warmed[:], in_=warm[:], func=EXP)
         load_logits(1, 0, 384)
         nc.sync.dma_start(out=v4_sb[:].bitcast(I32), in_=v4_words[0].bitcast(I32))
+        load_scales(nc.sync, 1, v8_scales)
         load_logits(0, 384, 512)
         load_v8(0)
         load_v8(1)

from contextlib import ExitStack

import concourse.mybir as mybir

T, J, D = 1024, 512, 1024
P = 128
PACK = 4
HALF = P * PACK
J_TILE = 128
N_TILE = 512

FLOPS = 2 * T * J * D

F32 = mybir.dt.float32
BF16 = mybir.dt.bfloat16
I32 = mybir.dt.int32
U32 = mybir.dt.uint32
U8 = mybir.dt.uint8
FP8X4 = mybir.dt.float8_e4m3fn_x4
FP4X4 = mybir.dt.float4_e2m1fn_x4
EXP = mybir.ActivationFunctionType.Exp
MULT = mybir.AluOpType.mult


def tile_mix_kvmix_tm_none_kernel(tc, lg, vs, v4_words, v4_scales, v8_words, v8_scales, out):
    nc = tc.nc
    j_tiles = J // J_TILE
    n_tiles = D // N_TILE

    with ExitStack() as ctx:
        keep = ctx.enter_context(tc.tile_pool(name="keep", bufs=1))
        psum = ctx.enter_context(tc.psum_pool(name="psum", bufs=1))
        ctx.enter_context(tc.manual_schedule())

        warm = keep.tile([P, 1], F32, name="warm")
        warmed = keep.tile([P, 1], F32, name="warmed")
        vs_sb = keep.tile([P, 2, PACK], F32, name="vs_sb")
        logits = [keep.tile([P, PACK, J], F32, name="logits%d" % h) for h in range(2)]
        exps = [keep.tile([P, PACK, J], F32, name="exps%d" % h) for h in range(2)]
        grouped = [keep.tile([P, J * PACK], BF16, name="grouped%d" % h, align_bytes=64) for h in range(2)]
        e_codes = [keep.tile([P, J], U32, name="e_codes%d" % h, align_bytes=64) for h in range(2)]
        e_scales = [keep.tile([P, J], U8, name="e_scales%d" % h, align_bytes=64) for h in range(2)]
        v4_sb = keep.tile([P, 2 * D], U8, name="v4_sb", align_bytes=64)
        v8_sb = keep.tile([P, D], U32, name="v8_sb", align_bytes=64)
        v_scales = [keep.tile([P, D], U8, name="v_scales%d" % h, align_bytes=64) for h in range(2)]
        results = [keep.tile([P, D], F32, name="results%d" % j) for j in range(j_tiles)]
        accs = [
            [psum.tile([P, N_TILE], F32, name="acc%d_%d" % (j, n)) for n in range(n_tiles)] for j in range(j_tiles)
        ]

        def load_logits(h, j0, j1):
            rows = lg[h * HALF : (h + 1) * HALF, j0:j1].rearrange("(p i) j -> p i j", i=PACK)
            nc.sync.dma_start(out=logits[h][:, :, j0:j1], in_=rows)

        def load_scales(engine, h, scales):
            for q in range(4):
                engine.dma_start(
                    out=v_scales[h][32 * q : 32 * q + 4, :].bitcast(I32),
                    in_=scales[0, 4 * q : 4 * q + 4, :].bitcast(I32),
                )

        nc.vector.memset(warm[:], 0.0)
        nc.vector.memset(v_scales[0][:].bitcast(I32), 0)
        nc.vector.memset(v_scales[1][:].bitcast(I32), 0)
        def load_v8(n):
            cols = slice(n * N_TILE, (n + 1) * N_TILE)
            nc.sync.dma_start(
                out=v8_sb[:, cols].bitcast(I32),
                in_=v8_words[0].rearrange("p n t -> p (n t)")[:, 4 * n * N_TILE : 4 * (n + 1) * N_TILE].bitcast(I32),
            )

        nc.scalar.dma_start(out=vs_sb[:], in_=vs.rearrange("(h p i) -> p h i", h=2, i=PACK))
        load_logits(0, 0, 384)
        load_scales(nc.scalar, 0, v4_scales)
        nc.scalar.activation(out=warmed[:], in_=warm[:], func=EXP)
        load_logits(1, 0, 384)
        nc.sync.dma_start(out=v4_sb[:].bitcast(I32), in_=v4_words[0].bitcast(I32))
        load_scales(nc.sync, 1, v8_scales)
        load_logits(0, 384, 512)
        load_v8(0)
        load_v8(1)
        load_logits(1, 384, 512)

        def cols(j0, j1, per=1):
            return slice(per * j0 * J_TILE, per * j1 * J_TILE)

        def exponentiate(h, j0, j1):
            nc.scalar.activation(out=exps[h][:, :, cols(j0, j1)], in_=logits[h][:, :, cols(j0, j1)], func=EXP)

        def scale(h, j0, j1):
            pairs = (j1 - j0) * J_TILE // 2
            factor = vs_sb[:, h, :].unsqueeze(1).unsqueeze(3).to_broadcast([P, pairs, PACK, 2])
            nc.vector.tensor_tensor(
                out=grouped[h][:, cols(j0, j1, PACK)].rearrange("p (c u i) -> p c i u", u=2, i=PACK),
                in0=exps[h][:, :, cols(j0, j1)].rearrange("p i (c u) -> p c i u", u=2),
                in1=factor,
                op=MULT,
            )

        def quantize(h, j0, j1):
            nc.vector.quantize_mx(
                out=e_codes[h][:, cols(j0, j1)].bitcast(FP8X4),
                scales=e_scales[h][:, cols(j0, j1)],
                in_=grouped[h][:, cols(j0, j1, PACK)],
            )

        def multiply(h, j0, j1):
            for j in range(j0, j1):
                for n in range(n_tiles):
                    if h == 0:
                        moving = v4_sb[:, 2 * n * N_TILE : 2 * (n + 1) * N_TILE].bitcast(FP4X4)
                    else:
                        moving = v8_sb[:, n * N_TILE : (n + 1) * N_TILE].bitcast(FP8X4)
                    nc.tensor.matmul_mx(
                        out=accs[j][n][:],
                        lhsT=e_codes[h][:, cols(j, j + 1)].bitcast(FP8X4),
                        lhsT_scale=e_scales[h][:, cols(j, j + 1)],
                        rhs=moving,
                        rhs_scale=v_scales[h][:, n * N_TILE : (n + 1) * N_TILE],
                        start=(h == 0),
                        stop=(h == 1),
                    )

        def drain(j, n, engine):
            d_cols = slice(n * N_TILE, (n + 1) * N_TILE)
            if engine == "scalar":
                nc.scalar.copy(out=results[j][:, d_cols], in_=accs[j][n][:])
            else:
                nc.vector.tensor_copy(out=results[j][:, d_cols], in_=accs[j][n][:])
            nc.sync.dma_start(out=out[j * J_TILE : (j + 1) * J_TILE, d_cols], in_=results[j][:, d_cols])

        exponentiate(0, 0, 1)
        exponentiate(0, 1, 2)
        scale(0, 0, 1)
        exponentiate(0, 2, 3)
        scale(0, 1, 2)
        quantize(0, 0, 1)
        multiply(0, 0, 1)
        exponentiate(1, 0, 1)
        scale(0, 2, 3)
        quantize(0, 1, 2)
        multiply(0, 1, 2)
        exponentiate(1, 1, 2)
        quantize(0, 2, 3)
        multiply(0, 2, 3)
        scale(1, 0, 1)
        exponentiate(1, 2, 3)
        scale(1, 1, 2)
        quantize(1, 0, 1)
        multiply(1, 0, 1)
        exponentiate(0, 3, 4)
        scale(1, 2, 3)
        quantize(1, 1, 2)
        multiply(1, 1, 2)
        drain(0, 0, "scalar")
        scale(0, 3, 4)
        quantize(1, 2, 3)
        multiply(1, 2, 3)
        drain(0, 1, "scalar")
        exponentiate(1, 3, 4)
        quantize(0, 3, 4)
        multiply(0, 3, 4)
        drain(1, 0, "vector")
        scale(1, 3, 4)
        drain(1, 1, "scalar")
        drain(2, 0, "vector")
        quantize(1, 3, 4)
        multiply(1, 3, 4)
        drain(2, 1, "scalar")
        drain(3, 0, "vector")
        drain(3, 1, "scalar")
